import numpy as np
import ml_dtypes


def mxq(x, axis, fmt="e4m3"):
    dtype, down = {"e4m3": (ml_dtypes.float8_e4m3fn, 7), "e5m2": (ml_dtypes.float8_e5m2, 14)}[fmt]
    v = np.moveaxis(np.asarray(x, np.float32).astype(ml_dtypes.bfloat16).astype(np.float64), axis, -1)
    blocks = v.reshape(v.shape[:-1] + (-1, 32))
    amax = np.abs(blocks).max(-1, keepdims=True)
    byte = np.maximum(np.where(amax > 0, np.frexp(amax)[1] - 1 + 127, 0) - down, 1)
    scale = np.exp2(byte - 127.0)
    codes = (blocks / scale).astype(np.float32).astype(dtype).astype(np.float64)
    return np.moveaxis((codes * scale).reshape(v.shape), -1, axis)


WIDE = False


def mx_kscale(k):
    if not WIDE:
        return np.ones(k)
    levels = np.array([10, -10, 5, -5, 0])
    if k % 512:
        return np.exp2(np.random.permutation(np.resize(levels, k // 32))).repeat(32)
    a = np.empty((k // 512, 16))
    for p in range(k // 512):
        a[p, :8] = np.random.permutation(np.resize(levels, 8))
        for g in range(8):
            far = levels[np.abs(levels - a[p, g]) >= 10]
            a[p, g + 8] = far[np.random.randint(len(far))]
    return np.exp2(a.ravel()).repeat(32)


def f64(x):
    return np.asarray(x).astype(np.float64)


def striped(idx):
    return np.tile(np.asarray(idx).reshape(-1, 16).T, (8, 1)).astype(np.uint16)


def unstriped(offs):
    return offs[:16].T.reshape(-1).astype(np.int64)


E2M1 = np.array([0.0, 0.5, 1.0, 1.5, 2.0, 3.0, 4.0, 6.0, -0.0, -0.5, -1.0, -1.5, -2.0, -3.0, -4.0, -6.0])


def pack_weight(w, fmt):
    k, n = w.shape
    w = f64(np.asarray(w, np.float32).astype(ml_dtypes.bfloat16)).reshape(k // 32, 32, n)
    amax = np.abs(w).max(1)
    if fmt == "e4m3":
        byte = np.frexp(amax)[1] - 1 + 127 - 7
    else:
        mant, ex = np.frexp(amax / 6.0)
        byte = np.where(mant > 0.5, ex, ex - 1) + 127
    byte = np.clip(np.where(amax > 0, byte, 1), 1, 254)
    scaled = (w * np.exp2(127.0 - byte)[:, None, :]).reshape(k, n).astype(np.float32)
    by_word = np.ascontiguousarray(scaled.reshape(k // 512, 128, 4, n).transpose(0, 1, 3, 2))
    if fmt == "e4m3":
        words = by_word.astype(ml_dtypes.float8_e4m3fn).view(np.uint8)
    else:
        c = by_word.astype(ml_dtypes.float4_e2m1fn).view(np.uint8) & 0xF
        words = (c[..., 0::2] | (c[..., 1::2] << 4)).reshape(k // 512, 128, 2 * n)
    return np.ascontiguousarray(words), np.ascontiguousarray(byte.astype(np.uint8).reshape(k // 512, 16, n))


def unpack_weight(words, scales, fmt):
    g, _, n = scales.shape
    words = np.ascontiguousarray(words).reshape(g, 128, n, -1)
    if fmt == "e4m3":
        vals = words.view(ml_dtypes.float8_e4m3fn).astype(np.float64)
    else:
        nib = np.empty((g, 128, n, 4), np.uint8)
        nib[..., 0::2] = words & 0xF
        nib[..., 1::2] = words >> 4
        vals = E2M1[nib]
    vals = vals * np.repeat(np.exp2(scales.astype(np.float64) - 127.0), 8, axis=1)[..., None]
    return vals.transpose(0, 1, 3, 2).reshape(g * 512, n)


D, T, I, Q, E, Z, X = 512, 2048, 512, 128, 512, 1024, 1024


def setup_inputs():
    n = np.random.standard_normal
    idx = np.random.permutation(T)[:I]
    idx2 = np.random.permutation(Z)[:I]
    idx3 = np.random.permutation(Z)[:I]
    idx4 = np.random.permutation(X)[:I]
    fd = mx_kscale(D)
    fi = mx_kscale(I)
    keysp = pack_weight(n((D, T)) / fd[:, None], "e4m3")
    return {
        "query": (n((D, Q)) * 1.0 / np.sqrt(D) * fd[:, None]).astype(np.float32),
        "keys_words": keysp[0],
        "keys_scales": keysp[1],
        "os": (np.random.uniform(0.02, 0.08, (1, I)) * fi).astype(np.float32),
        "vals": (n((E, T))).astype(np.float32),
        "vals2": (n((E, X))).astype(np.float32),
        "vsc": (np.random.uniform(0.5, 2.0, (1, I)) / fi).astype(np.float32),
        "offs": striped(idx),
        "offs2": striped(idx2),
        "offs3": striped(idx3),
        "offs4": striped(idx4),
    }


def reference(query, keys_words, keys_scales, os, vals, vals2, vsc, offs, offs2, offs3, offs4):
    idx = unstriped(offs)
    idx2 = unstriped(offs2)
    idx3 = unstriped(offs3)
    idx4 = unstriped(offs4)
    keysu = unpack_weight(keys_words, keys_scales, "e4m3")
    queryq = mxq(f64(query), 0, "e4m3")
    keysidxg = keysu[:, idx]
    a = queryq.T @ keysidxg
    f0 = np.zeros((Q, Z))
    f0[:, idx2] = a
    w = a + f0[:, idx3]
    wo1 = w * f64(os)
    wt1 = wo1.T
    vz = np.maximum(f64(vals)[:, idx], f64(vals2)[:, idx4]) * f64(vsc)
    vt1 = vz.T
    wt1q = mxq(wt1, 0, "e4m3")
    vt1q = mxq(vt1, 0, "e4m3")
    o = wt1q.T @ vt1q
    return o

@@ -1,0 +1,221 @@
+from contextlib import ExitStack
+
+import concourse.mybir as mybir
+from concourse.masks import make_identity
+
+D, T, I, Q, E, Z, X = 512, 2048, 512, 128, 512, 1024, 1024
+FLOPS = 2 * Q * I * D + 2 * Q * E * I
+
+F32 = mybir.dt.float32
+BF16 = mybir.dt.bfloat16
+I32 = mybir.dt.int32
+U32 = mybir.dt.uint32
+U16 = mybir.dt.uint16
+U8 = mybir.dt.uint8
+FP8X4 = mybir.dt.float8_e4m3fn_x4
+COPY = mybir.ActivationFunctionType.Copy
+ADD = mybir.AluOpType.add
+MULT = mybir.AluOpType.mult
+MAX = mybir.AluOpType.max
+
+P = 128
+PACK = 4
+RUN = 8
+GROUPS = I // (PACK * RUN)
+LIST_COLS = I // 16
+E_TILES = E // P
+
+
+def tile_attend_passedthrough_mergedvalues_lean_kernel(
+    tc, query, keys_words, keys_scales, weight_factor, vals, vals2, value_factor, offs, offs2, offs3, offs4, out
+):
+    nc = tc.nc
+    with ExitStack() as ctx:
+        sb = ctx.enter_context(tc.tile_pool(name="sb", bufs=1))
+        ps = ctx.enter_context(tc.psum_pool(name="ps", bufs=1))
+
+        def dealt(ap, groups):
+            return ap.rearrange("p (g t r) -> p t g r", g=groups, t=PACK)
+
+        key_list = sb.tile([P, LIST_COLS], U16, name="key_list")
+        put_list = sb.tile([P, LIST_COLS], U16, name="put_list")
+        get_list = sb.tile([P, LIST_COLS], U16, name="get_list")
+        second_list = sb.tile([P, LIST_COLS], U16, name="second_list")
+        pool_words = sb.tile([P, T], U32, name="pool_words")
+        pool_scales = sb.tile([P, T], U8, name="pool_scales")
+        query_rows = sb.tile([P, PACK, Q], F32, name="query_rows")
+        factor_rows = sb.tile([P, P], F32, name="factor_rows")
+        places = sb.tile([P, Z], F32, name="places")
+        identity = sb.tile([P, P], F32, name="identity")
+        first_store = [sb.tile([P, T], F32, name="first_store%d" % b) for b in range(E_TILES)]
+        second_store = [sb.tile([P, X], F32, name="second_store%d" % b) for b in range(E_TILES)]
+
+        nc.gpsimd.memset(pool_scales[:].bitcast(I32), 0)
+        nc.vector.memset(factor_rows[:], 0.0)
+        nc.vector.memset(places[:], 0.0)
+        make_identity(nc, identity[:])
+
+        def load_first(b):
+            nc.sync.dma_start(out=first_store[b][:], in_=vals[b * P : (b + 1) * P, :])
+
+        def load_second(b):
+            nc.sync.dma_start(out=second_store[b][:], in_=vals2[b * P : (b + 1) * P, :])
+
+        nc.sync.dma_start(key_list[:], offs)
+        nc.sync.dma_start(
+            out=pool_words[:].bitcast(I32), in_=keys_words[0].rearrange("p n t -> p (n t)").bitcast(I32)
+        )
+        for quadrant in range(4):
+            nc.scalar.dma_start(
+                out=pool_scales[32 * quadrant : 32 * quadrant + 4, :].bitcast(I32),
+                in_=keys_scales[0, 4 * quadrant : 4 * quadrant + 4, :].bitcast(I32),
+            )
+        nc.sync.dma_start(out=query_rows[:], in_=query.rearrange("(p t) q -> p t q", t=PACK))
+        nc.sync.dma_start(second_list[:], offs4)
+        load_second(0)
+        nc.sync.dma_start(put_list[:], offs2)
+        load_first(0)
+        for first_row, factor in ((0, weight_factor), (PACK, value_factor)):
+            nc.sync.dma_start(
+                out=factor_rows[first_row : first_row + PACK, :].rearrange("t (g r) -> t g r", r=RUN),
+                in_=factor.rearrange("o (g t r) -> (o t) g r", t=PACK, r=RUN),
+            )
+        load_second(1)
+        load_first(1)
+        nc.sync.dma_start(get_list[:], offs3)
+        load_second(2)
+        load_first(2)
+        load_first(E_TILES - 1)
+        load_second(E_TILES - 1)
+
+        key_scales = sb.tile([P, I], U8, name="key_scales", align_bytes=64)
+        key_words = sb.tile([P, I], U32, name="key_words", align_bytes=64)
+        nc.vector.tensor_copy(key_scales[:], pool_scales[:].indirect(key_list[:]))
+        nc.vector.tensor_copy(key_words[:], pool_words[:].indirect(key_list[:]))
+        query_bf = sb.tile([P, Q, PACK], BF16, name="query_bf", align_bytes=64)
+        nc.scalar.copy(query_bf[:], query_rows[:].rearrange("p t q -> p q t"))
+        query_words = sb.tile([P, Q], U32, name="query_words", align_bytes=64)
+        query_scales = sb.tile([P, Q], U8, name="query_scales", align_bytes=64)
+        nc.vector.quantize_mx(
+            out=query_words[:].bitcast(FP8X4), scales=query_scales[:], in_=query_bf[:].rearrange("p q t -> p (q t)")
+        )
+        score_bank = ps.tile([P, I], F32, name="score_bank")
+        nc.tensor.matmul_mx(
+            out=score_bank[:],
+            lhsT=query_words[:].bitcast(FP8X4),
+            lhsT_scale=query_scales[:],
+            rhs=key_words[:].bitcast(FP8X4),
+            rhs_scale=key_scales[:],
+            start=True,
+            stop=True,
+        )
+        scores = sb.tile([P, I], F32, name="scores")
+        nc.vector.tensor_copy(scores[:], score_bank[:])
+
+        picked_first = [sb.tile([P, I], F32, name="picked_first%d" % b, tag="picked_first%d" % b, align_bytes=64) for b in range(E_TILES)]
+        picked_second = [sb.tile([P, I], F32, name="picked_second%d" % b) for b in range(E_TILES)]
+
+        def gather(on_vector, picked, store, slot_list, lo, hi):
+            window = store[:].indirect(slot_list[:, lo // 16 : hi // 16])
+            if on_vector:
+                nc.vector.tensor_copy(picked[:, lo:hi], window)
+            else:
+                nc.scalar.activation(picked[:, lo:hi], window, COPY)
+
+        gather(False, picked_second[0], second_store[0], second_list, 0, I)
+        for half in range(2):
+            lo, hi = half * I // 2, (half + 1) * I // 2
+            nc.scalar.activation(places[:].indirect(put_list[:, lo // 16 : hi // 16]), scores[:, lo:hi], COPY)
+
+        factor_bank = ps.tile([P, P], F32, name="factor_bank")
+        nc.tensor.transpose(factor_bank[:], factor_rows[:], identity[:])
+        factors = sb.tile([P, 2 * PACK], F32, name="factors")
+        nc.vector.tensor_copy(factors[:], factor_bank[:, 0 : 2 * PACK])
+
+        def turn(source, name, tag, bufs):
+            bank = ps.tile([P, PACK, P], F32, name=name, tag=tag, bufs=bufs)
+            for t in range(PACK):
+                nc.tensor.transpose(bank[:, t, :], source[:, t, :], identity[:])
+            return bank
+
+        def scale_and_round(bank, first_col, name, tag):
+            rounded = sb.tile([P, P, PACK], BF16, name=name, tag=tag, align_bytes=64)
+            factor_view = factors[:, first_col : first_col + PACK].unsqueeze(1).to_broadcast([P, P, PACK])
+            nc.vector.tensor_tensor(rounded[:], bank[:].rearrange("p t c -> p c t"), factor_view, MULT)
+            return rounded
+
+        def quantize(rounded, name):
+            words = sb.tile([P, P], U32, name=name + "_words", align_bytes=64)
+            scales = sb.tile([P, P], U8, name=name + "_scales", align_bytes=64)
+            nc.vector.quantize_mx(
+                out=words[:].bitcast(FP8X4), scales=scales[:], in_=rounded[:].rearrange("p c t -> p (c t)")
+            )
+            return words, scales
+
+        def larger(merged, b, lo, hi):
+            g0, g1 = lo // (PACK * RUN), hi // (PACK * RUN)
+            nc.vector.tensor_tensor(
+                merged[:].rearrange("p t (g r) -> p t g r", r=RUN)[:, :, g0:g1, :],
+                dealt(picked_first[b][:, lo:hi], g1 - g0),
+                dealt(picked_second[b][:, lo:hi], g1 - g0),
+                MAX,
+            )
+
+        merged = [sb.tile([P, PACK, P], F32, name="merged%d" % b) for b in range(E_TILES)]
+
+        def turn_values(b):
+            return turn(merged[b], "value_bank%d" % b, "value_bank", 2)
+
+        def finish_values(bank, b, tag):
+            return quantize(scale_and_round(bank, PACK, "value_bf%d" % b, tag), "value%d" % b)
+
+        gather(True, picked_first[0], first_store[0], key_list, 0, I)
+        larger(merged[0], 0, 0, I)
+        gather(True, picked_second[1], second_store[1], second_list, 0, I)
+        value_mx = [finish_values(turn_values(0), 0, "value_bf0")]
+
+        looked_up = sb.tile([P, I], F32, name="looked_up")
+        nc.vector.tensor_copy(looked_up[:], places[:].indirect(get_list[:]))
+        weights = sb.tile([P, PACK, P], F32, name="weights")
+        nc.vector.tensor_tensor(
+            weights[:].rearrange("p t (g r) -> p t g r", r=RUN), dealt(looked_up[:], GROUPS), dealt(scores[:], GROUPS), ADD
+        )
+        weight_bank = turn(weights, "weight_bank", "weight_bank", 1)
+        weight_words, weight_scales = quantize(scale_and_round(weight_bank, 0, "weight_bf", "weight_bf"), "weight")
+
+        gather(False, picked_first[1], first_store[1], key_list, 0, I)
+        larger(merged[1], 1, 0, I)
+        value_mx.append(finish_values(turn_values(1), 1, "value_bf1"))
+
+        gather(False, picked_second[2], second_store[2], second_list, 0, I)
+        gather(False, picked_first[2], first_store[2], key_list, 0, I)
+        larger(merged[2], 2, 0, I)
+        bank2 = turn_values(2)
+
+        gather(False, picked_first[3], first_store[3], key_list, 0, I)
+        gather(True, picked_second[3], second_store[3], second_list, 0, I // 2)
+        gather(False, picked_second[3], second_store[3], second_list, I // 2, I)
+        larger(merged[3], 3, 0, I // 2)
+        larger(merged[3], 3, I // 2, I)
+        bank3 = turn_values(3)
+        value_mx.append(finish_values(bank2, 2, "picked_first3"))
+        value_mx.append(finish_values(bank3, 3, "value_bf3"))
+
+        def product(blocks, name):
+            bank = ps.tile([P, len(blocks) * P], F32, name=name + "_bank")
+            for j, b in enumerate(blocks):
+                nc.tensor.matmul_mx(
+                    out=bank[:, j * P : (j + 1) * P],
+                    lhsT=weight_words[:].bitcast(FP8X4),
+                    lhsT_scale=weight_scales[:],
+                    rhs=value_mx[b][0][:].bitcast(FP8X4),
+                    rhs_scale=value_mx[b][1][:],
+                    start=True,
+                    stop=True,
+                )
+            result = sb.tile([P, len(blocks) * P], F32, name=name)
+            nc.scalar.copy(result[:], bank[:])
+            nc.sync.dma_start(out=out[:, blocks[0] * P : (blocks[-1] + 1) * P], in_=result[:])
+
+        product(list(range(E_TILES - 1)), "early")
+        product([E_TILES - 1], "last")

@@ -61,19 +61,20 @@ def tile_attend_passedthrough_mergedvalues_lean_kernel(
         def load_second(b):
             nc.sync.dma_start(out=second_store[b][:], in_=vals2[b * P : (b + 1) * P, :])
 
+        nc.sync.dma_start(out=query_rows[:], in_=query.rearrange("(p t) q -> p t q", t=PACK))
+        for quadrant in range(4):
+            nc.sync.dma_start(
+                out=pool_scales[32 * quadrant : 32 * quadrant + 4, :].bitcast(I32),
+                in_=keys_scales[0, 4 * quadrant : 4 * quadrant + 4, :].bitcast(I32),
+            )
         nc.sync.dma_start(key_list[:], offs)
         nc.sync.dma_start(
             out=pool_words[:].bitcast(I32), in_=keys_words[0].rearrange("p n t -> p (n t)").bitcast(I32)
         )
-        for quadrant in range(4):
-            nc.scalar.dma_start(
-                out=pool_scales[32 * quadrant : 32 * quadrant + 4, :].bitcast(I32),
-                in_=keys_scales[0, 4 * quadrant : 4 * quadrant + 4, :].bitcast(I32),
-            )
-        nc.sync.dma_start(out=query_rows[:], in_=query.rearrange("(p t) q -> p t q", t=PACK))
-        nc.sync.dma_start(second_list[:], offs4)
         load_second(0)
         nc.sync.dma_start(put_list[:], offs2)
+        nc.sync.dma_start(second_list[:], offs4)
+        nc.sync.dma_start(get_list[:], offs3)
         load_first(0)
         for first_row, factor in ((0, weight_factor), (PACK, value_factor)):
             nc.sync.dma_start(
@@ -82,7 +83,6 @@ def tile_attend_passedthrough_mergedvalues_lean_kernel(
             )
         load_second(1)
         load_first(1)
-        nc.sync.dma_start(get_list[:], offs3)
         load_second(2)
         load_first(2)
         load_first(E_TILES - 1)
@@ -91,7 +91,6 @@ def tile_attend_passedthrough_mergedvalues_lean_kernel(
         key_scales = sb.tile([P, I], U8, name="key_scales", align_bytes=64)
         key_words = sb.tile([P, I], U32, name="key_words", align_bytes=64)
         nc.vector.tensor_copy(key_scales[:], pool_scales[:].indirect(key_list[:]))
-        nc.vector.tensor_copy(key_words[:], pool_words[:].indirect(key_list[:]))
         query_bf = sb.tile([P, Q, PACK], BF16, name="query_bf", align_bytes=64)
         nc.scalar.copy(query_bf[:], query_rows[:].rearrange("p t q -> p q t"))
         query_words = sb.tile([P, Q], U32, name="query_words", align_bytes=64)
@@ -99,18 +98,22 @@ def tile_attend_passedthrough_mergedvalues_lean_kernel(
         nc.vector.quantize_mx(
             out=query_words[:].bitcast(FP8X4), scales=query_scales[:], in_=query_bf[:].rearrange("p q t -> p (q t)")
         )
-        score_bank = ps.tile([P, I], F32, name="score_bank")
-        nc.tensor.matmul_mx(
-            out=score_bank[:],
-            lhsT=query_words[:].bitcast(FP8X4),
-            lhsT_scale=query_scales[:],
-            rhs=key_words[:].bitcast(FP8X4),
-            rhs_scale=key_scales[:],
-            start=True,
-            stop=True,
-        )
         scores = sb.tile([P, I], F32, name="scores")
-        nc.vector.tensor_copy(scores[:], score_bank[:])
+        for half in range(2):
+            lo, hi = half * I // 2, (half + 1) * I // 2
+            nc.vector.tensor_copy(key_words[:, lo:hi], pool_words[:].indirect(key_list[:, lo // 16 : hi // 16]))
+            score_bank = ps.tile([P, I // 2], F32, name="score_bank%d" % half)
+            nc.tensor.matmul_mx(
+                out=score_bank[:],
+                lhsT=query_words[:].bitcast(FP8X4),
+                lhsT_scale=query_scales[:],
+                rhs=key_words[:, lo:hi].bitcast(FP8X4),
+                rhs_scale=key_scales[:, lo:hi],
+                start=True,
+                stop=True,
+            )
+            nc.scalar.copy(scores[:, lo:hi], score_bank[:])
+            nc.scalar.activation(places[:].indirect(put_list[:, lo // 16 : hi // 16]), scores[:, lo:hi], COPY)
 
         picked_first = [sb.tile([P, I], F32, name="picked_first%d" % b, tag="picked_first%d" % b, align_bytes=64) for b in range(E_TILES)]
         picked_second = [sb.tile([P, I], F32, name="picked_second%d" % b) for b in range(E_TILES)]
@@ -122,10 +125,7 @@ def tile_attend_passedthrough_mergedvalues_lean_kernel(
             else:
                 nc.scalar.activation(picked[:, lo:hi], window, COPY)
 
-        gather(False, picked_second[0], second_store[0], second_list, 0, I)
-        for half in range(2):
-            lo, hi = half * I // 2, (half + 1) * I // 2
-            nc.scalar.activation(places[:].indirect(put_list[:, lo // 16 : hi // 16]), scores[:, lo:hi], COPY)
+        gather(True, picked_second[0], second_store[0], second_list, 0, I)
 
         factor_bank = ps.tile([P, P], F32, name="factor_bank")
         nc.tensor.transpose(factor_bank[:], factor_rows[:], identity[:])
@@ -152,12 +152,11 @@ def tile_attend_passedthrough_mergedvalues_lean_kernel(
             )
             return words, scales
 
-        def larger(merged, b, lo, hi):
-            g0, g1 = lo // (PACK * RUN), hi // (PACK * RUN)
+        def larger(merged, b, t0, t1):
             nc.vector.tensor_tensor(
-                merged[:].rearrange("p t (g r) -> p t g r", r=RUN)[:, :, g0:g1, :],
-                dealt(picked_first[b][:, lo:hi], g1 - g0),
-                dealt(picked_second[b][:, lo:hi], g1 - g0),
+                merged[:, t0:t1, :].rearrange("p t (g r) -> p t g r", r=RUN),
+                dealt(picked_first[b][:], GROUPS)[:, t0:t1],
+                dealt(picked_second[b][:], GROUPS)[:, t0:t1],
                 MAX,
             )
 
@@ -170,38 +169,38 @@ def tile_attend_passedthrough_mergedvalues_lean_kernel(
             return quantize(scale_and_round(bank, PACK, "value_bf%d" % b, tag), "value%d" % b)
 
         gather(True, picked_first[0], first_store[0], key_list, 0, I)
-        larger(merged[0], 0, 0, I)
+        larger(merged[0], 0, 0, PACK)
         gather(True, picked_second[1], second_store[1], second_list, 0, I)
         value_mx = [finish_values(turn_values(0), 0, "value_bf0")]
 
         looked_up = sb.tile([P, I], F32, name="looked_up")
-        nc.vector.tensor_copy(looked_up[:], places[:].indirect(get_list[:]))
-        weights = sb.tile([P, PACK, P], F32, name="weights")
+        gather(False, looked_up, places, get_list, 0, I)
+        weights = sb.tile([P, PACK, P], F32, name="weights", tag="value_bf0", align_bytes=64)
         nc.vector.tensor_tensor(
             weights[:].rearrange("p t (g r) -> p t g r", r=RUN), dealt(looked_up[:], GROUPS), dealt(scores[:], GROUPS), ADD
         )
         weight_bank = turn(weights, "weight_bank", "weight_bank", 1)
-        weight_words, weight_scales = quantize(scale_and_round(weight_bank, 0, "weight_bf", "weight_bf"), "weight")
 
         gather(False, picked_first[1], first_store[1], key_list, 0, I)
-        larger(merged[1], 1, 0, I)
+        larger(merged[1], 1, 0, PACK)
+        weight_words, weight_scales = quantize(scale_and_round(weight_bank, 0, "weight_bf", "picked_first1"), "weight")
         value_mx.append(finish_values(turn_values(1), 1, "value_bf1"))
 
         gather(False, picked_second[2], second_store[2], second_list, 0, I)
         gather(False, picked_first[2], first_store[2], key_list, 0, I)
-        larger(merged[2], 2, 0, I)
+        larger(merged[2], 2, 0, PACK)
         bank2 = turn_values(2)
 
         gather(False, picked_first[3], first_store[3], key_list, 0, I)
         gather(True, picked_second[3], second_store[3], second_list, 0, I // 2)
         gather(False, picked_second[3], second_store[3], second_list, I // 2, I)
-        larger(merged[3], 3, 0, I // 2)
-        larger(merged[3], 3, I // 2, I)
+        larger(merged[3], 3, 0, 2)
+        larger(merged[3], 3, 2, PACK)
         bank3 = turn_values(3)
         value_mx.append(finish_values(bank2, 2, "picked_first3"))
         value_mx.append(finish_values(bank3, 3, "value_bf3"))
 
-        def product(blocks, name):
+        def product(blocks, name, copy_out):
             bank = ps.tile([P, len(blocks) * P], F32, name=name + "_bank")
             for j, b in enumerate(blocks):
                 nc.tensor.matmul_mx(
@@ -214,8 +213,8 @@ def tile_attend_passedthrough_mergedvalues_lean_kernel(
                     stop=True,
                 )
             result = sb.tile([P, len(blocks) * P], F32, name=name)
-            nc.scalar.copy(result[:], bank[:])
+            copy_out(result[:], bank[:])
             nc.sync.dma_start(out=out[:, blocks[0] * P : (blocks[-1] + 1) * P], in_=result[:])
 
-        product(list(range(E_TILES - 1)), "early")
-        product([E_TILES - 1], "last")
+        product(list(range(E_TILES - 1)), "early", nc.scalar.copy)
+        product([E_TILES - 1], "last", nc.vector.tensor_copy)

@@ -63,7 +63,7 @@ def tile_attend_passedthrough_mergedvalues_lean_kernel(
 
         nc.sync.dma_start(out=query_rows[:], in_=query.rearrange("(p t) q -> p t q", t=PACK))
         for quadrant in range(4):
-            nc.sync.dma_start(
+            (nc.scalar if quadrant < 2 else nc.sync).dma_start(
                 out=pool_scales[32 * quadrant : 32 * quadrant + 4, :].bitcast(I32),
                 in_=keys_scales[0, 4 * quadrant : 4 * quadrant + 4, :].bitcast(I32),
             )
@@ -112,11 +112,11 @@ def tile_attend_passedthrough_mergedvalues_lean_kernel(
                 start=True,
                 stop=True,
             )
-            nc.scalar.copy(scores[:, lo:hi], score_bank[:])
+            nc.vector.tensor_copy(scores[:, lo:hi], score_bank[:])
             nc.scalar.activation(places[:].indirect(put_list[:, lo // 16 : hi // 16]), scores[:, lo:hi], COPY)
 
         picked_first = [sb.tile([P, I], F32, name="picked_first%d" % b, tag="picked_first%d" % b, align_bytes=64) for b in range(E_TILES)]
-        picked_second = [sb.tile([P, I], F32, name="picked_second%d" % b) for b in range(E_TILES)]
+        picked_second = [sb.tile([P, I], F32, name="picked_second%d" % b, tag="picked_second%d" % b) for b in range(E_TILES)]
 
         def gather(on_vector, picked, store, slot_list, lo, hi):
             window = store[:].indirect(slot_list[:, lo // 16 : hi // 16])
@@ -127,7 +127,7 @@ def tile_attend_passedthrough_mergedvalues_lean_kernel(
 
         gather(True, picked_second[0], second_store[0], second_list, 0, I)
 
-        factor_bank = ps.tile([P, P], F32, name="factor_bank")
+        factor_bank = ps.tile([P, P], F32, name="factor_bank", tag="weight_bank")
         nc.tensor.transpose(factor_bank[:], factor_rows[:], identity[:])
         factors = sb.tile([P, 2 * PACK], F32, name="factors")
         nc.vector.tensor_copy(factors[:], factor_bank[:, 0 : 2 * PACK])
@@ -191,7 +191,8 @@ def tile_attend_passedthrough_mergedvalues_lean_kernel(
         larger(merged[2], 2, 0, PACK)
         bank2 = turn_values(2)
 
-        gather(False, picked_first[3], first_store[3], key_list, 0, I)
+        gather(True, picked_first[3], first_store[3], key_list, 0, I // 4)
+        gather(False, picked_first[3], first_store[3], key_list, I // 4, I)
         gather(True, picked_second[3], second_store[3], second_list, 0, I // 2)
         gather(False, picked_second[3], second_store[3], second_list, I // 2, I)
         larger(merged[3], 3, 0, 2)
@@ -200,7 +201,7 @@ def tile_attend_passedthrough_mergedvalues_lean_kernel(
         value_mx.append(finish_values(bank2, 2, "picked_first3"))
         value_mx.append(finish_values(bank3, 3, "value_bf3"))
 
-        def product(blocks, name, copy_out):
+        def product(blocks, name, copy_out, tag):
             bank = ps.tile([P, len(blocks) * P], F32, name=name + "_bank")
             for j, b in enumerate(blocks):
                 nc.tensor.matmul_mx(
@@ -212,9 +213,10 @@ def tile_attend_passedthrough_mergedvalues_lean_kernel(
                     start=True,
                     stop=True,
                 )
-            result = sb.tile([P, len(blocks) * P], F32, name=name)
+            result = sb.tile([P, len(blocks) * P], F32, name=name, tag=tag)
             copy_out(result[:], bank[:])
             nc.sync.dma_start(out=out[:, blocks[0] * P : (blocks[-1] + 1) * P], in_=result[:])
 
-        product(list(range(E_TILES - 1)), "early", nc.scalar.copy)
-        product([E_TILES - 1], "last", nc.vector.tensor_copy)
+        product([0, 1], "early", nc.scalar.copy, "picked_second3")
+        product([2], "third", nc.scalar.copy, "third")
+        product([3], "last", nc.vector.tensor_copy, "last")

from contextlib import ExitStack

import concourse.mybir as mybir
from concourse.masks import make_identity

D, T, I, Q, E, Z, X = 512, 2048, 512, 128, 512, 1024, 1024
FLOPS = 2 * Q * I * D + 2 * Q * E * I

F32 = mybir.dt.float32
BF16 = mybir.dt.bfloat16
I32 = mybir.dt.int32
U32 = mybir.dt.uint32
U16 = mybir.dt.uint16
U8 = mybir.dt.uint8
FP8X4 = mybir.dt.float8_e4m3fn_x4
COPY = mybir.ActivationFunctionType.Copy
ADD = mybir.AluOpType.add
MULT = mybir.AluOpType.mult
MAX = mybir.AluOpType.max

P = 128
PACK = 4
RUN = 8
GROUPS = I // (PACK * RUN)
LIST_COLS = I // 16
E_TILES = E // P


def tile_attend_passedthrough_mergedvalues_lean_kernel(
    tc, query, keys_words, keys_scales, weight_factor, vals, vals2, value_factor, offs, offs2, offs3, offs4, out
):
    nc = tc.nc
    with ExitStack() as ctx:
        sb = ctx.enter_context(tc.tile_pool(name="sb", bufs=1))
        ps = ctx.enter_context(tc.psum_pool(name="ps", bufs=1))

        def dealt(ap, groups):
            return ap.rearrange("p (g t r) -> p t g r", g=groups, t=PACK)

        key_list = sb.tile([P, LIST_COLS], U16, name="key_list")
        put_list = sb.tile([P, LIST_COLS], U16, name="put_list")
        get_list = sb.tile([P, LIST_COLS], U16, name="get_list")
        second_list = sb.tile([P, LIST_COLS], U16, name="second_list")
        pool_words = sb.tile([P, T], U32, name="pool_words")
        pool_scales = sb.tile([P, T], U8, name="pool_scales")
        query_rows = sb.tile([P, PACK, Q], F32, name="query_rows")
        factor_rows = sb.tile([P, P], F32, name="factor_rows")
        places = sb.tile([P, Z], F32, name="places")
        identity = sb.tile([P, P], F32, name="identity")
        first_store = [sb.tile([P, T], F32, name="first_store%d" % b) for b in range(E_TILES)]
        second_store = [sb.tile([P, X], F32, name="second_store%d" % b) for b in range(E_TILES)]

        nc.gpsimd.memset(pool_scales[:].bitcast(I32), 0)
        nc.vector.memset(factor_rows[:], 0.0)
        nc.vector.memset(places[:], 0.0)
        make_identity(nc, identity[:])

        def load_first(b):
            nc.sync.dma_start(out=first_store[b][:], in_=vals[b * P : (b + 1) * P, :])

        def load_second(b):
            nc.sync.dma_start(out=second_store[b][:], in_=vals2[b * P : (b + 1) * P, :])

        nc.sync.dma_start(out=query_rows[:], in_=query.rearrange("(p t) q -> p t q", t=PACK))
        for quadrant in range(4):
            (nc.scalar if quadrant < 2 else nc.sync).dma_start(
                out=pool_scales[32 * quadrant : 32 * quadrant + 4, :].bitcast(I32),
                in_=keys_scales[0, 4 * quadrant : 4 * quadrant + 4, :].bitcast(I32),
            )
        nc.sync.dma_start(key_list[:], offs)
        nc.sync.dma_start(
            out=pool_words[:].bitcast(I32), in_=keys_words[0].rearrange("p n t -> p (n t)").bitcast(I32)
        )
        load_second(0)
        nc.sync.dma_start(put_list[:], offs2)
        nc.sync.dma_start(second_list[:], offs4)
        nc.sync.dma_start(get_list[:], offs3)
        load_first(0)
        for first_row, factor in ((0, weight_factor), (PACK, value_factor)):
            nc.sync.dma_start(
                out=factor_rows[first_row : first_row + PACK, :].rearrange("t (g r) -> t g r", r=RUN),
                in_=factor.rearrange("o (g t r) -> (o t) g r", t=PACK, r=RUN),
            )
        load_second(1)
        load_first(1)
        load_second(2)
        load_first(2)
        load_first(E_TILES - 1)
        load_second(E_TILES - 1)

        key_scales = sb.tile([P, I], U8, name="key_scales", align_bytes=64)
        key_words = sb.tile([P, I], U32, name="key_words", align_bytes=64)
        nc.vector.tensor_copy(key_scales[:], pool_scales[:].indirect(key_list[:]))
        query_bf = sb.tile([P, Q, PACK], BF16, name="query_bf", align_bytes=64)
        nc.scalar.copy(query_bf[:], query_rows[:].rearrange("p t q -> p q t"))
        query_words = sb.tile([P, Q], U32, name="query_words", align_bytes=64)
        query_scales = sb.tile([P, Q], U8, name="query_scales", align_bytes=64)
        nc.vector.quantize_mx(
            out=query_words[:].bitcast(FP8X4), scales=query_scales[:], in_=query_bf[:].rearrange("p q t -> p (q t)")
        )
        scores = sb.tile([P, I], F32, name="scores")
        for half in range(2):
            lo, hi = half * I // 2, (half + 1) * I // 2
            nc.vector.tensor_copy(key_words[:, lo:hi], pool_words[:].indirect(key_list[:, lo // 16 : hi // 16]))
            score_bank = ps.tile([P, I // 2], F32, name="score_bank%d" % half)
            nc.tensor.matmul_mx(
                out=score_bank[:],
                lhsT=query_words[:].bitcast(FP8X4),
                lhsT_scale=query_scales[:],
                rhs=key_words[:, lo:hi].bitcast(FP8X4),
                rhs_scale=key_scales[:, lo:hi],
                start=True,
                stop=True,
            )
            nc.vector.tensor_copy(scores[:, lo:hi], score_bank[:])
            nc.scalar.activation(places[:].indirect(put_list[:, lo // 16 : hi // 16]), scores[:, lo:hi], COPY)

        picked_first = [sb.tile([P, I], F32, name="picked_first%d" % b, tag="picked_first%d" % b, align_bytes=64) for b in range(E_TILES)]
        picked_second = [sb.tile([P, I], F32, name="picked_second%d" % b, tag="picked_second%d" % b) for b in range(E_TILES)]

        def gather(on_vector, picked, store, slot_list, lo, hi):
            window = store[:].indirect(slot_list[:, lo // 16 : hi // 16])
            if on_vector:
                nc.vector.tensor_copy(picked[:, lo:hi], window)
            else:
                nc.scalar.activation(picked[:, lo:hi], window, COPY)

        gather(True, picked_second[0], second_store[0], second_list, 0, I)

        factor_bank = ps.tile([P, P], F32, name="factor_bank", tag="weight_bank")
        nc.tensor.transpose(factor_bank[:], factor_rows[:], identity[:])
        factors = sb.tile([P, 2 * PACK], F32, name="factors")
        nc.vector.tensor_copy(factors[:], factor_bank[:, 0 : 2 * PACK])

        def turn(source, name, tag, bufs):
            bank = ps.tile([P, PACK, P], F32, name=name, tag=tag, bufs=bufs)
            for t in range(PACK):
                nc.tensor.transpose(bank[:, t, :], source[:, t, :], identity[:])
            return bank

        def scale_and_round(bank, first_col, name, tag):
            rounded = sb.tile([P, P, PACK], BF16, name=name, tag=tag, align_bytes=64)
            factor_view = factors[:, first_col : first_col + PACK].unsqueeze(1).to_broadcast([P, P, PACK])
            nc.vector.tensor_tensor(rounded[:], bank[:].rearrange("p t c -> p c t"), factor_view, MULT)
            return rounded

        def quantize(rounded, name):
            words = sb.tile([P, P], U32, name=name + "_words", align_bytes=64)
            scales = sb.tile([P, P], U8, name=name + "_scales", align_bytes=64)
            nc.vector.quantize_mx(
                out=words[:].bitcast(FP8X4), scales=scales[:], in_=rounded[:].rearrange("p c t -> p (c t)")
            )
            return words, scales

        def larger(merged, b, t0, t1):
            nc.vector.tensor_tensor(
                merged[:, t0:t1, :].rearrange("p t (g r) -> p t g r", r=RUN),
                dealt(picked_first[b][:], GROUPS)[:, t0:t1],
                dealt(picked_second[b][:], GROUPS)[:, t0:t1],
                MAX,
            )

        merged = [sb.tile([P, PACK, P], F32, name="merged%d" % b) for b in range(E_TILES)]

        def turn_values(b):
            return turn(merged[b], "value_bank%d" % b, "value_bank", 2)

        def finish_values(bank, b, tag):
            return quantize(scale_and_round(bank, PACK, "value_bf%d" % b, tag), "value%d" % b)

        gather(True, picked_first[0], first_store[0], key_list, 0, I)
        larger(merged[0], 0, 0, PACK)
        gather(True, picked_second[1], second_store[1], second_list, 0, I)
        value_mx = [finish_values(turn_values(0), 0, "value_bf0")]

        looked_up = sb.tile([P, I], F32, name="looked_up")
        gather(False, looked_up, places, get_list, 0, I)
        weights = sb.tile([P, PACK, P], F32, name="weights", tag="value_bf0", align_bytes=64)
        nc.vector.tensor_tensor(
            weights[:].rearrange("p t (g r) -> p t g r", r=RUN), dealt(looked_up[:], GROUPS), dealt(scores[:], GROUPS), ADD
        )
        weight_bank = turn(weights, "weight_bank", "weight_bank", 1)

        gather(False, picked_first[1], first_store[1], key_list, 0, I)
        larger(merged[1], 1, 0, PACK)
        weight_words, weight_scales = quantize(scale_and_round(weight_bank, 0, "weight_bf", "picked_first1"), "weight")
        value_mx.append(finish_values(turn_values(1), 1, "value_bf1"))

        gather(False, picked_second[2], second_store[2], second_list, 0, I)
        gather(False, picked_first[2], first_store[2], key_list, 0, I)
        larger(merged[2], 2, 0, PACK)
        bank2 = turn_values(2)

        gather(True, picked_first[3], first_store[3], key_list, 0, I // 4)
        gather(False, picked_first[3], first_store[3], key_list, I // 4, I)
        gather(True, picked_second[3], second_store[3], second_list, 0, I // 2)
        gather(False, picked_second[3], second_store[3], second_list, I // 2, I)
        larger(merged[3], 3, 0, 2)
        larger(merged[3], 3, 2, PACK)
        bank3 = turn_values(3)
        value_mx.append(finish_values(bank2, 2, "picked_first3"))
        value_mx.append(finish_values(bank3, 3, "value_bf3"))

        def product(blocks, name, copy_out, tag):
            bank = ps.tile([P, len(blocks) * P], F32, name=name + "_bank")
            for j, b in enumerate(blocks):
                nc.tensor.matmul_mx(
                    out=bank[:, j * P : (j + 1) * P],
                    lhsT=weight_words[:].bitcast(FP8X4),
                    lhsT_scale=weight_scales[:],
                    rhs=value_mx[b][0][:].bitcast(FP8X4),
                    rhs_scale=value_mx[b][1][:],
                    start=True,
                    stop=True,
                )
            result = sb.tile([P, len(blocks) * P], F32, name=name, tag=tag)
            copy_out(result[:], bank[:])
            nc.sync.dma_start(out=out[:, blocks[0] * P : (blocks[-1] + 1) * P], in_=result[:])

        product([0, 1], "early", nc.scalar.copy, "picked_second3")
        product([2], "third", nc.scalar.copy, "third")
        product([3], "last", nc.vector.tensor_copy, "last")
